import numpy as np
import ml_dtypes


def mxq(x, axis, fmt="e4m3"):
    dtype, down = {"e4m3": (ml_dtypes.float8_e4m3fn, 7), "e5m2": (ml_dtypes.float8_e5m2, 14)}[fmt]
    v = np.moveaxis(np.asarray(x, np.float32).astype(ml_dtypes.bfloat16).astype(np.float64), axis, -1)
    blocks = v.reshape(v.shape[:-1] + (-1, 32))
    amax = np.abs(blocks).max(-1, keepdims=True)
    byte = np.maximum(np.where(amax > 0, np.frexp(amax)[1] - 1 + 127, 0) - down, 1)
    scale = np.exp2(byte - 127.0)
    codes = (blocks / scale).astype(np.float32).astype(dtype).astype(np.float64)
    return np.moveaxis((codes * scale).reshape(v.shape), -1, axis)


WIDE = False


def mx_kscale(k):
    if not WIDE:
        return np.ones(k)
    levels = np.array([10, -10, 5, -5, 0])
    if k % 512:
        return np.exp2(np.random.permutation(np.resize(levels, k // 32))).repeat(32)
    a = np.empty((k // 512, 16))
    for p in range(k // 512):
        a[p, :8] = np.random.permutation(np.resize(levels, 8))
        for g in range(8):
            far = levels[np.abs(levels - a[p, g]) >= 10]
            a[p, g + 8] = far[np.random.randint(len(far))]
    return np.exp2(a.ravel()).repeat(32)


def f64(x):
    return np.asarray(x).astype(np.float64)


def striped(idx):
    return np.tile(idx.reshape(-1, 16).T, (8, 1)).astype(np.uint16)


def unstriped(offs):
    return offs[:16].T.reshape(-1).astype(np.int64)


def striped8(idx):
    return np.concatenate([x.reshape(-1, 16).T for x in idx]).astype(np.uint16)


def runs(offs, k):
    lists = np.stack([offs[16 * r : 16 * r + 16].T.reshape(-1) for r in range(8)]).astype(np.int64)
    return lists[np.arange(k) % 512 // 64]


def pack_weight(w):
    k, n = w.shape
    w = f64(np.asarray(w, np.float32).astype(ml_dtypes.bfloat16)).reshape(k // 32, 32, n)
    amax = np.abs(w).max(1)
    byte = np.clip(np.where(amax > 0, np.frexp(amax)[1] - 1 + 127 - 7, 1), 1, 254)
    scaled = (w * np.exp2(127.0 - byte)[:, None, :]).reshape(k, n).astype(np.float32)
    words = np.ascontiguousarray(scaled.reshape(k // 512, 128, 4, n).transpose(0, 1, 3, 2)).astype(ml_dtypes.float8_e4m3fn).view(np.uint8)
    return words, np.ascontiguousarray(byte.astype(np.uint8).reshape(k // 512, 16, n))


def unpack_weight(words, scales):
    g, p, n, _ = words.shape
    vals = np.ascontiguousarray(words).view(ml_dtypes.float8_e4m3fn).astype(np.float64) * np.repeat(np.exp2(scales.astype(np.float64) - 127.0), 8, axis=1)[..., None]
    return vals.transpose(0, 1, 3, 2).reshape(g * 512, n)


def sigmoid(v):
    return 1.0 / (1.0 + np.exp(-np.maximum(v, -700.0)))


K, T, S, N, H = 512, 2048, 512, 512, 512


def setup_inputs():
    n = np.random.standard_normal
    s = mx_kscale(K)[:, None]
    u = mx_kscale(H)
    packed_xT = pack_weight(n((K, T)) * s)
    return {
        "x_words": packed_xT[0],
        "x_scales": packed_xT[1],
        "w1": (n((K, H)) / np.sqrt(K) / s).astype(np.float32),
        "w2": (n((K, H)) / np.sqrt(K) / s).astype(np.float32),
        "gn": (np.random.uniform(0.5, 1.5, (H, 1)) * u[:, None]).astype(np.float32),
        "gm": (np.random.uniform(0.5, 1.5, (H, 1)) * u[:, None]).astype(np.float32),
        "w3": (n((H, N)) / np.sqrt(2 * H) / u[:, None]).astype(np.float32),
        "w4": (n((H, N)) / np.sqrt(2 * H) / u[:, None]).astype(np.float32),
        "offs": striped(np.random.permutation(T)[:S]),
        "hz": striped8(np.random.randint(0, T, (8, S))),
        "n1": striped8(np.stack([np.random.permutation(S) for _ in range(8)])),
        "n2": striped8(np.stack([np.random.permutation(S) for _ in range(8)])),
        "n3": striped(np.random.permutation(S)),
        "n4": striped(np.random.permutation(S)),
        "n5": striped8(np.stack([np.random.permutation(S) for _ in range(8)])),
    }


def reference(x_words, x_scales, w1, w2, gn, gm, w3, w4, offs, hz, n1, n2, n3, n4, n5):
    xq = unpack_weight(x_words, x_scales)[:, unstriped(offs)]
    y = mxq(f64(w1), 0, "e4m3").T @ xq
    z = f64(gn) * (y * (sigmoid(y[np.arange(H)[:, None], runs(n1, H)] - (y[np.arange(H)[:, None], runs(n2, H)]))))
    x_hz = unpack_weight(x_words, x_scales)[np.arange(K)[:, None], runs(hz, K)]
    d = mxq(f64(w2), 0, "e4m3").T @ x_hz
    z2 = f64(gm) * (np.minimum(np.maximum(d, d[:, unstriped(n3)]), d[:, unstriped(n4)]))
    h = mxq(f64(w3), 0, "e4m3").T @ mxq(z, 0, "e4m3") + mxq(f64(w4), 0, "e4m3").T @ mxq(z2, 0, "e4m3")
    return h - (h[np.arange(N)[:, None], runs(n5, N)])

@@ -1,0 +1,261 @@
+from contextlib import ExitStack
+
+import concourse.mybir as mybir
+
+K, T, S, N, H = 512, 2048, 512, 512, 512
+FLOPS = 4 * 2 * 512 * 512 * 512
+
+F32 = mybir.dt.float32
+BF16 = mybir.dt.bfloat16
+I32 = mybir.dt.int32
+U32 = mybir.dt.uint32
+U16 = mybir.dt.uint16
+U8 = mybir.dt.uint8
+FP8X4 = mybir.dt.float8_e4m3fn_x4
+ALU = mybir.AluOpType
+ACT = mybir.ActivationFunctionType
+
+P = 128
+PACK = 4
+HALF = S // 2
+FUSED = (0, 2)
+TAIL = ((0, 0, 1), (1, 0, 0), (0, 256, 1), (1, 256, 0), (3, 0, 0), (2, 0, 1), (3, 256, 0), (2, 256, 0))
+PIECES = ((0, 256), (256, 128), (384, 128))
+
+
+def tile_picked_hjoincmpminmxdif_none_p_kernel(
+    tc, x_words, x_scales, w1, w2, gn, gm, w3, w4, offs, hz, n1, n2, n3, n4, n5, out
+):
+    nc = tc.nc
+    with ExitStack() as ctx:
+        keep = ctx.enter_context(tc.tile_pool(name="keep", bufs=1))
+        psum = ctx.enter_context(tc.psum_pool(name="psum", bufs=1))
+
+        def sb(name, shape, dtype):
+            return keep.tile(shape, dtype, name=name, align_bytes=64)
+
+        def load_list(name, src):
+            lst = sb(name, [P, S // 16], U16)
+            nc.sync.dma_start(lst[:], src)
+            return lst
+
+        def entries(lst, start, count):
+            return lst[:, start // 16 : (start + count) // 16]
+
+        def load_weight(name, w, c0, cols):
+            raw = sb(name, [P, PACK, cols], F32)
+            nc.sync.dma_start(out=raw[:], in_=w.rearrange("(p j) c -> p j c", j=PACK)[:, :, c0 : c0 + cols])
+            return raw
+
+        xs = sb("xs", [P, T], U8)
+        nc.vector.memset(xs[:].bitcast(I32), 0)
+        l_offs = load_list("l_offs", offs)
+        l_hz = load_list("l_hz", hz)
+        w1_raw = [load_weight("w1_raw0", w1, 0, HALF)]
+        rows = x_scales[0].bitcast(I32)
+        for r in range(2):
+            nc.sync.dma_start(out=xs[r:P:16, :].bitcast(I32), in_=rows[r:16:2, :])
+        for r in range(2, 4):
+            nc.sync.dma_start(out=xs[r:P:32, :].bitcast(I32), in_=rows[r:16:4, :])
+        w1_raw.append(load_weight("w1_raw1", w1, HALF, HALF))
+        xw = sb("xw", [P, T], I32)
+        nc.sync.dma_start(out=xw[:], in_=x_words[0].rearrange("p n t -> p (n t)").bitcast(I32))
+        w2_raw = [load_weight("w2_raw0", w2, 0, HALF)]
+        l_n2 = load_list("l_n2", n2)
+        w2_raw.append(load_weight("w2_raw1", w2, HALF, HALF))
+
+        def weight_tiles(name):
+            staged = [sb("%s_bf%d" % (name, u), [P, 2, P, PACK], BF16) for u in range(2)]
+            return staged, sb(name + "_codes", [P, 512], U32), sb(name + "_scales", [P, 512], U8)
+
+        def cast_weight(copy, wt, raw, u, m0):
+            count = raw.shape[2] // PACK
+            copy(
+                out=wt[0][u][:, :, m0 : m0 + count, :].rearrange("p t m j -> p m j t"),
+                in_=raw[:].rearrange("p j (m t) -> p m j t", t=PACK)[:, :, :, 2 * u : 2 * u + 2],
+            )
+
+        def quant_weight(wt, u):
+            cols = slice(u * 256, (u + 1) * 256)
+            nc.vector.quantize_mx(
+                out=wt[1][:, cols].bitcast(FP8X4), scales=wt[2][:, cols],
+                in_=wt[0][u][:].rearrange("p t m j -> p (t m j)"),
+            )
+
+        def product(acc, wt, t, codes, scales, start, stop):
+            cols = slice(t * P, (t + 1) * P)
+            nc.tensor.matmul_mx(
+                out=acc, lhsT=wt[1][:, cols].bitcast(FP8X4), lhsT_scale=wt[2][:, cols],
+                rhs=codes.bitcast(FP8X4), rhs_scale=scales, start=start, stop=stop,
+            )
+
+        xq_w = sb("xq_w", [P, S], U32)
+        xq_s = sb("xq_s", [P, S], U8)
+        xh_w = sb("xh_w", [P, S], U32)
+        xh_g = sb("xh_g", [P, S], U8)
+        xh_s = sb("xh_s", [P, S], U8)
+        nc.vector.tensor_copy(xq_s[:], xs[:].indirect(l_offs[:]))
+        nc.vector.tensor_copy(xh_g[:], xs[:].indirect(l_hz[:]))
+        wt1 = weight_tiles("w1")
+        for q in range(2):
+            for u in range(2):
+                cast_weight(nc.scalar.copy, wt1, w1_raw[q], u, 64 * q)
+        quant_weight(wt1, 0)
+        nc.vector.tensor_copy(xh_s[:].bitcast(I32), xh_g[:].bitcast(I32))
+        quant_weight(wt1, 1)
+        banks = [psum.tile([P, S], F32, name="y_ps%d" % t, tag="bank%d" % t) for t in range(PACK)]
+        nc.vector.tensor_copy(xq_w[:], xw[:].bitcast(U32).indirect(l_offs[:]))
+        for t in range(PACK):
+            product(banks[t][:], wt1, t, xq_w[:], xq_s[:], True, True)
+        nc.vector.tensor_copy(xh_w[:], xw[:].bitcast(U32).indirect(l_hz[:]))
+        for r in range(2):
+            nc.sync.dma_start(out=xh_s[2 + r : P : 32, :].bitcast(I32), in_=xh_g[16 + r : P : 32, :].bitcast(I32))
+        gn_sb = sb("gn_sb", [P, PACK], F32)
+        gm_sb = sb("gm_sb", [P, PACK], F32)
+        l_n1 = load_list("l_n1", n1)
+        nc.sync.dma_start(out=gm_sb[:], in_=gm.rearrange("(p t) o -> p (t o)", t=PACK))
+        nc.sync.dma_start(out=gn_sb[:], in_=gn.rearrange("(p t) o -> p (t o)", t=PACK))
+        w3_raw = load_weight("w3_raw", w3, 0, N)
+        l_n3 = load_list("l_n3", n3)
+        l_n4 = load_list("l_n4", n4)
+        w4_raw = load_weight("w4_raw", w4, 0, N)
+        l_n5 = load_list("l_n5", n5)
+
+        gm_abs = sb("gm_abs", [P, PACK], F32)
+        gm_sign = sb("gm_sign", [P, PACK], BF16)
+        nc.scalar.activation(gm_abs[:], gm_sb[:], ACT.Abs)
+        nc.scalar.activation(gm_sign[:], gm_sb[:], ACT.Sign)
+
+        wt2 = weight_tiles("w2")
+        for q in range(2):
+            for u in range(2):
+                cast_weight(nc.vector.tensor_copy, wt2, w2_raw[q], u, 64 * q)
+        quant_weight(wt2, 0)
+        quant_weight(wt2, 1)
+        d_ps = [psum.tile([P, S], F32, name="d_ps%d" % t, tag="bank%d" % (PACK + t)) for t in range(PACK)]
+        for t in range(PACK):
+            product(d_ps[t][:], wt2, t, xh_w[:], xh_s[:], True, True)
+
+        y_sb = [sb("y_sb%d" % t, [P, 2 * S], F32) for t in range(PACK)]
+        y2 = [sb("y2_%d" % t, [P, S], F32) for t in range(PACK)]
+        diff = [sb("diff%d" % t, [P, S], F32) for t in range(PACK)]
+        sig = [sb("sig%d" % t, [P, S], F32) for t in range(PACK)]
+        z_planes = sb("z_planes", [P, PACK, S], BF16)
+        d_sb = [sb("d_sb%d" % t, [P, S], F32) for t in range(PACK)]
+
+        def fetch_y(t):
+            (nc.vector.tensor_copy if t >= 2 else nc.scalar.copy)(out=y_sb[t][:, :S], in_=banks[t][:])
+            nc.scalar.activation(y2[t][:], y_sb[t][:].indirect(l_n2[:]), ACT.Copy)
+            nc.vector.tensor_tensor(diff[t][:], y_sb[t][:].indirect(l_n1[:]), y2[t][:], ALU.subtract)
+
+        def gate_y(t):
+            nc.scalar.activation(sig[t][:], diff[t][:], ACT.Sigmoid)
+            nc.vector.scalar_tensor_tensor(
+                z_planes[:, t, :], banks[t][:], gn_sb[:, t : t + 1], sig[t][:], ALU.mult, ALU.mult
+            )
+
+        def leave_d(t):
+            nc.scalar.activation(d_sb[t][:], d_ps[t][:], ACT.Copy, scale=gm_abs[:, t : t + 1])
+
+        for t in range(PACK):
+            fetch_y(t)
+        for t in range(PACK):
+            gate_y(t)
+            leave_d(t)
+
+        z_codes = sb("z_codes", [P, S], U32)
+        z_scales = sb("z_scales", [P, S], U8)
+        wt3 = weight_tiles("w3")
+        wt4 = weight_tiles("w4")
+        for wt, raw in ((wt3, w3_raw), (wt4, w4_raw)):
+            for u in range(2):
+                cast_weight(nc.vector.tensor_copy, wt, raw, u, 0)
+            for u in range(2):
+                quant_weight(wt, u)
+
+        h_neg = [sb("h_neg%d" % t, [P, S], F32) for t in range(PACK)]
+        h_pos = {t: sb("h_pos%d" % t, [P, S], F32) for t in FUSED}
+        z2_codes = sb("z2_codes", [P, S], U32)
+        z2_scales = sb("z2_scales", [P, S], U8)
+        h_ps = {}
+        free_banks = [0, 1, 2, 3, 4, 5]
+
+        def make_z2(c0, width):
+            cols = slice(c0, c0 + width)
+            d3 = sb("d3_%d" % c0, [P, PACK, width], F32)
+            d4 = sb("d4_%d" % c0, [P, PACK, width], F32)
+            big = sb("big_%d" % c0, [P, PACK, width], F32)
+            woven = sb("z2_woven%d" % c0, [P, width, PACK], BF16)
+            signed = sb("z2_signed%d" % c0, [P, width, PACK], BF16)
+            for t in range(PACK):
+                nc.scalar.activation(d3[:, t, :], d_sb[t][:].indirect(entries(l_n3, c0, width)), ACT.Copy)
+                nc.vector.scalar_tensor_tensor(
+                    big[:, t, :], d_ps[t][:, cols], gm_abs[:, t : t + 1], d3[:, t, :], ALU.mult, ALU.max
+                )
+            for t in range(PACK):
+                nc.scalar.activation(d4[:, t, :], d_sb[t][:].indirect(entries(l_n4, c0, width)), ACT.Copy)
+            nc.vector.tensor_tensor(
+                woven[:].rearrange("p (c i) t -> p c t i", i=2),
+                big[:].rearrange("p t (c i) -> p c t i", i=2),
+                d4[:].rearrange("p t (c i) -> p c t i", i=2),
+                ALU.min,
+            )
+            z_woven = sb("z_woven%d" % c0, [P, width, PACK], BF16)
+            nc.vector.tensor_copy(
+                out=z_woven[:].rearrange("p (c i) t -> p c t i", i=4),
+                in_=z_planes[:, :, cols].rearrange("p t (c i) -> p c t i", i=4),
+            )
+            nc.vector.tensor_tensor(
+                signed[:], woven[:], gm_sign[:].unsqueeze(1).to_broadcast([P, width, PACK]), ALU.mult
+            )
+            nc.vector.quantize_mx(
+                out=z_codes[:, cols].bitcast(FP8X4), scales=z_scales[:, cols],
+                in_=z_woven[:].rearrange("p j t -> p (j t)"),
+            )
+            nc.vector.quantize_mx(
+                out=z2_codes[:, cols].bitcast(FP8X4), scales=z2_scales[:, cols],
+                in_=signed[:].rearrange("p j t -> p (j t)"),
+            )
+            for pair in ((0, 2), (1, 3)):
+                bank = psum.tile([P, 2, width], F32, name="h_ps%d_%d" % (c0, pair[0]), tag="bank%d" % free_banks.pop(0))
+                for k, t in enumerate(pair):
+                    product(bank[:, k, :], wt3, t, z_codes[:, cols], z_scales[:, cols], k == 0, False)
+                for k, t in enumerate(pair):
+                    product(bank[:, k, :], wt4, t, z2_codes[:, cols], z2_scales[:, cols], False, k == 1)
+                    h_ps[c0, t] = bank[:, k, :]
+
+        def leave_h(c0, width, last):
+            cols = slice(c0, c0 + width)
+            for t in (0, 2, 1, 3):
+                if last and t in FUSED:
+                    nc.vector.tensor_scalar(h_neg[t][:, cols], h_ps[c0, t], -1.0, None, ALU.mult)
+                else:
+                    nc.scalar.activation(h_neg[t][:, cols], h_ps[c0, t], ACT.Copy, scale=-1.0)
+
+        def double_h(c0, width):
+            cols = slice(c0, c0 + width)
+            for t in FUSED:
+                nc.vector.tensor_scalar(h_pos[t][:, cols], h_neg[t][:, cols], -1.0, None, ALU.mult)
+
+        for piece in PIECES:
+            make_z2(*piece)
+        for piece in PIECES[:-1]:
+            leave_h(*piece, False)
+        for c0, width in PIECES[:-1]:
+            for t in FUSED:
+                nc.scalar.copy(out=h_pos[t][:, c0 : c0 + width], in_=h_ps[c0, t])
+        leave_h(*PIECES[-1], True)
+        double_h(*PIECES[-1])
+
+        out_rows = out.rearrange("(p t) n -> p t n", t=PACK)
+        for t, c0, fused in TAIL:
+            res = sb("res%d_%d" % (t, c0), [P, HALF], F32)
+            cols = slice(c0, c0 + HALF)
+            fetched = h_neg[t][:].indirect(entries(l_n5, c0, HALF))
+            if fused:
+                nc.vector.tensor_tensor(res[:], fetched, h_pos[t][:, cols], ALU.add)
+            else:
+                h5 = sb("h5_%d_%d" % (t, c0), [P, HALF], F32)
+                nc.scalar.activation(h5[:], fetched, ACT.Copy)
+                nc.vector.tensor_tensor(res[:], h5[:], h_neg[t][:, cols], ALU.subtract)
+            nc.sync.dma_start(out=out_rows[:, t, cols], in_=res[:])

@@ -63,6 +63,9 @@ def tile_picked_hjoincmpminmxdif_none_p_kernel(
         w2_raw = [load_weight("w2_raw0", w2, 0, HALF)]
         l_n2 = load_list("l_n2", n2)
         w2_raw.append(load_weight("w2_raw1", w2, HALF, HALF))
+        warm = sb("warm", [P, 2], F32)
+        nc.gpsimd.memset(warm[:, 0:1], 0.0)
+        nc.scalar.activation(warm[:, 1:2], warm[:, 0:1], ACT.Sigmoid)
 
         def weight_tiles(name):
             staged = [sb("%s_bf%d" % (name, u), [P, 2, P, PACK], BF16) for u in range(2)]

@@ -18,8 +18,8 @@ ACT = mybir.ActivationFunctionType
 P = 128
 PACK = 4
 HALF = S // 2
-FUSED = (0, 2)
-TAIL = ((0, 0, 1), (1, 0, 0), (0, 256, 1), (1, 256, 0), (3, 0, 0), (2, 0, 1), (3, 256, 0), (2, 256, 0))
+YV = (2, 3)
+ZS = ()
 PIECES = ((0, 256), (256, 128), (384, 128))
 
 
@@ -58,10 +58,10 @@ def tile_picked_hjoincmpminmxdif_none_p_kernel(
         for r in range(2, 4):
             nc.sync.dma_start(out=xs[r:P:32, :].bitcast(I32), in_=rows[r:16:4, :])
         w1_raw.append(load_weight("w1_raw1", w1, HALF, HALF))
+        l_n2 = load_list("l_n2", n2)
         xw = sb("xw", [P, T], I32)
         nc.sync.dma_start(out=xw[:], in_=x_words[0].rearrange("p n t -> p (n t)").bitcast(I32))
         w2_raw = [load_weight("w2_raw0", w2, 0, HALF)]
-        l_n2 = load_list("l_n2", n2)
         w2_raw.append(load_weight("w2_raw1", w2, HALF, HALF))
         warm = sb("warm", [P, 2], F32)
         nc.gpsimd.memset(warm[:, 0:1], 0.0)
@@ -107,9 +107,17 @@ def tile_picked_hjoincmpminmxdif_none_p_kernel(
         nc.vector.tensor_copy(xh_s[:].bitcast(I32), xh_g[:].bitcast(I32))
         quant_weight(wt1, 1)
         banks = [psum.tile([P, S], F32, name="y_ps%d" % t, tag="bank%d" % t) for t in range(PACK)]
-        nc.vector.tensor_copy(xq_w[:], xw[:].bitcast(U32).indirect(l_offs[:]))
-        for t in range(PACK):
+        y_ps = {t: [] for t in range(PACK)}
+        for half in range(2):
+            cols = slice(half * HALF, (half + 1) * HALF)
+            nc.vector.tensor_copy(xq_w[:, cols], xw[:].bitcast(U32).indirect(entries(l_offs, half * HALF, HALF)))
+            for t in range(2):
+                acc = banks[half][:, t * HALF : (t + 1) * HALF]
+                product(acc, wt1, t, xq_w[:, cols], xq_s[:, cols], True, True)
+                y_ps[t].append((cols, acc))
+        for t in range(2, PACK):
             product(banks[t][:], wt1, t, xq_w[:], xq_s[:], True, True)
+            y_ps[t].append((slice(0, S), banks[t][:]))
         nc.vector.tensor_copy(xh_w[:], xw[:].bitcast(U32).indirect(l_hz[:]))
         for r in range(2):
             nc.sync.dma_start(out=xh_s[2 + r : P : 32, :].bitcast(I32), in_=xh_g[16 + r : P : 32, :].bitcast(I32))
@@ -147,19 +155,24 @@ def tile_picked_hjoincmpminmxdif_none_p_kernel(
         d_sb = [sb("d_sb%d" % t, [P, S], F32) for t in range(PACK)]
 
         def fetch_y(t):
-            (nc.vector.tensor_copy if t >= 2 else nc.scalar.copy)(out=y_sb[t][:, :S], in_=banks[t][:])
+            if t >= 2:
+                (nc.vector.tensor_copy if t in YV else nc.scalar.copy)(out=y_sb[t][:, :S], in_=banks[t][:])
             nc.scalar.activation(y2[t][:], y_sb[t][:].indirect(l_n2[:]), ACT.Copy)
             nc.vector.tensor_tensor(diff[t][:], y_sb[t][:].indirect(l_n1[:]), y2[t][:], ALU.subtract)
 
         def gate_y(t):
             nc.scalar.activation(sig[t][:], diff[t][:], ACT.Sigmoid)
             nc.vector.scalar_tensor_tensor(
-                z_planes[:, t, :], banks[t][:], gn_sb[:, t : t + 1], sig[t][:], ALU.mult, ALU.mult
+                z_planes[:, t, :], y_sb[t][:, :S], gn_sb[:, t : t + 1], sig[t][:], ALU.mult, ALU.mult
             )
 
         def leave_d(t):
             nc.scalar.activation(d_sb[t][:], d_ps[t][:], ACT.Copy, scale=gm_abs[:, t : t + 1])
 
+        for half in range(2):
+            for t in range(2):
+                cols, acc = y_ps[t][half]
+                nc.scalar.copy(out=y_sb[t][:, cols], in_=acc)
         for t in range(PACK):
             fetch_y(t)
         for t in range(PACK):
@@ -177,11 +190,11 @@ def tile_picked_hjoincmpminmxdif_none_p_kernel(
                 quant_weight(wt, u)
 
         h_neg = [sb("h_neg%d" % t, [P, S], F32) for t in range(PACK)]
-        h_pos = {t: sb("h_pos%d" % t, [P, S], F32) for t in FUSED}
+        h_twin = [sb("h_twin%d" % t, [P, HALF], F32) for t in range(PACK)]
         z2_codes = sb("z2_codes", [P, S], U32)
         z2_scales = sb("z2_scales", [P, S], U8)
         h_ps = {}
-        free_banks = [0, 1, 2, 3, 4, 5]
+        free_banks = [0, 1, 2, 3, 4, 5, 6, 7]
 
         def make_z2(c0, width):
             cols = slice(c0, c0 + width)
@@ -204,7 +217,7 @@ def tile_picked_hjoincmpminmxdif_none_p_kernel(
                 ALU.min,
             )
             z_woven = sb("z_woven%d" % c0, [P, width, PACK], BF16)
-            nc.vector.tensor_copy(
+            (nc.scalar.copy if c0 in ZS else nc.vector.tensor_copy)(
                 out=z_woven[:].rearrange("p (c i) t -> p c t i", i=4),
                 in_=z_planes[:, :, cols].rearrange("p t (c i) -> p c t i", i=4),
             )
@@ -219,46 +232,32 @@ def tile_picked_hjoincmpminmxdif_none_p_kernel(
                 out=z2_codes[:, cols].bitcast(FP8X4), scales=z2_scales[:, cols],
                 in_=signed[:].rearrange("p j t -> p (j t)"),
             )
-            for pair in ((0, 2), (1, 3)):
-                bank = psum.tile([P, 2, width], F32, name="h_ps%d_%d" % (c0, pair[0]), tag="bank%d" % free_banks.pop(0))
+            for pair in ((0, 1), (2, 3)) if c0 + width < S else ((0,), (1,), (2,), (3,)):
+                bank = psum.tile([P, len(pair), width], F32, name="h_ps%d_%d" % (c0, pair[0]), tag="bank%d" % free_banks.pop(0))
                 for k, t in enumerate(pair):
                     product(bank[:, k, :], wt3, t, z_codes[:, cols], z_scales[:, cols], k == 0, False)
                 for k, t in enumerate(pair):
-                    product(bank[:, k, :], wt4, t, z2_codes[:, cols], z2_scales[:, cols], False, k == 1)
+                    product(bank[:, k, :], wt4, t, z2_codes[:, cols], z2_scales[:, cols], False, k == len(pair) - 1)
                     h_ps[c0, t] = bank[:, k, :]
 
-        def leave_h(c0, width, last):
-            cols = slice(c0, c0 + width)
-            for t in (0, 2, 1, 3):
-                if last and t in FUSED:
-                    nc.vector.tensor_scalar(h_neg[t][:, cols], h_ps[c0, t], -1.0, None, ALU.mult)
-                else:
-                    nc.scalar.activation(h_neg[t][:, cols], h_ps[c0, t], ACT.Copy, scale=-1.0)
-
-        def double_h(c0, width):
-            cols = slice(c0, c0 + width)
-            for t in FUSED:
-                nc.vector.tensor_scalar(h_pos[t][:, cols], h_neg[t][:, cols], -1.0, None, ALU.mult)
+        def leave_h(c0, width):
+            for t in range(PACK):
+                nc.scalar.activation(h_neg[t][:, c0 : c0 + width], h_ps[c0, t], ACT.Copy, scale=-1.0)
 
         for piece in PIECES:
             make_z2(*piece)
-        for piece in PIECES[:-1]:
-            leave_h(*piece, False)
-        for c0, width in PIECES[:-1]:
-            for t in FUSED:
-                nc.scalar.copy(out=h_pos[t][:, c0 : c0 + width], in_=h_ps[c0, t])
-        leave_h(*PIECES[-1], True)
-        double_h(*PIECES[-1])
+        for piece in PIECES:
+            leave_h(*piece)
+        for t in range(PACK):
+            nc.sync.dma_start(out=h_twin[t][:], in_=h_neg[t][:, :HALF])
 
         out_rows = out.rearrange("(p t) n -> p t n", t=PACK)
-        for t, c0, fused in TAIL:
-            res = sb("res%d_%d" % (t, c0), [P, HALF], F32)
-            cols = slice(c0, c0 + HALF)
-            fetched = h_neg[t][:].indirect(entries(l_n5, c0, HALF))
-            if fused:
-                nc.vector.tensor_tensor(res[:], fetched, h_pos[t][:, cols], ALU.add)
-            else:
-                h5 = sb("h5_%d_%d" % (t, c0), [P, HALF], F32)
-                nc.scalar.activation(h5[:], fetched, ACT.Copy)
-                nc.vector.tensor_tensor(res[:], h5[:], h_neg[t][:, cols], ALU.subtract)
-            nc.sync.dma_start(out=out_rows[:, t, cols], in_=res[:])
+        for t in range(PACK):
+            low = sb("low%d" % t, [P, HALF], F32)
+            high = sb("high%d" % t, [P, HALF], F32)
+            h5 = sb("h5_%d" % t, [P, HALF], F32)
+            nc.vector.tensor_tensor(low[:], h_neg[t][:].indirect(entries(l_n5, 0, HALF)), h_twin[t][:], ALU.subtract)
+            nc.sync.dma_start(out=out_rows[:, t, :HALF], in_=low[:])
+            nc.scalar.activation(h5[:], h_neg[t][:].indirect(entries(l_n5, HALF, HALF)), ACT.Copy)
+            nc.vector.tensor_tensor(high[:], h5[:], h_neg[t][:, HALF:], ALU.subtract)
+            nc.sync.dma_start(out=out_rows[:, t, HALF:], in_=high[:])

from contextlib import ExitStack

import concourse.mybir as mybir

K, T, S, N, H = 512, 2048, 512, 512, 512
FLOPS = 4 * 2 * 512 * 512 * 512

F32 = mybir.dt.float32
BF16 = mybir.dt.bfloat16
I32 = mybir.dt.int32
U32 = mybir.dt.uint32
U16 = mybir.dt.uint16
U8 = mybir.dt.uint8
FP8X4 = mybir.dt.float8_e4m3fn_x4
ALU = mybir.AluOpType
ACT = mybir.ActivationFunctionType

P = 128
PACK = 4
HALF = S // 2
YV = (2, 3)
ZS = ()
PIECES = ((0, 256), (256, 128), (384, 128))


def tile_picked_hjoincmpminmxdif_none_p_kernel(
    tc, x_words, x_scales, w1, w2, gn, gm, w3, w4, offs, hz, n1, n2, n3, n4, n5, out
):
    nc = tc.nc
    with ExitStack() as ctx:
        keep = ctx.enter_context(tc.tile_pool(name="keep", bufs=1))
        psum = ctx.enter_context(tc.psum_pool(name="psum", bufs=1))

        def sb(name, shape, dtype):
            return keep.tile(shape, dtype, name=name, align_bytes=64)

        def load_list(name, src):
            lst = sb(name, [P, S // 16], U16)
            nc.sync.dma_start(lst[:], src)
            return lst

        def entries(lst, start, count):
            return lst[:, start // 16 : (start + count) // 16]

        def load_weight(name, w, c0, cols):
            raw = sb(name, [P, PACK, cols], F32)
            nc.sync.dma_start(out=raw[:], in_=w.rearrange("(p j) c -> p j c", j=PACK)[:, :, c0 : c0 + cols])
            return raw

        xs = sb("xs", [P, T], U8)
        nc.vector.memset(xs[:].bitcast(I32), 0)
        l_offs = load_list("l_offs", offs)
        l_hz = load_list("l_hz", hz)
        w1_raw = [load_weight("w1_raw0", w1, 0, HALF)]
        rows = x_scales[0].bitcast(I32)
        for r in range(2):
            nc.sync.dma_start(out=xs[r:P:16, :].bitcast(I32), in_=rows[r:16:2, :])
        for r in range(2, 4):
            nc.sync.dma_start(out=xs[r:P:32, :].bitcast(I32), in_=rows[r:16:4, :])
        w1_raw.append(load_weight("w1_raw1", w1, HALF, HALF))
        l_n2 = load_list("l_n2", n2)
        xw = sb("xw", [P, T], I32)
        nc.sync.dma_start(out=xw[:], in_=x_words[0].rearrange("p n t -> p (n t)").bitcast(I32))
        w2_raw = [load_weight("w2_raw0", w2, 0, HALF)]
        w2_raw.append(load_weight("w2_raw1", w2, HALF, HALF))
        warm = sb("warm", [P, 2], F32)
        nc.gpsimd.memset(warm[:, 0:1], 0.0)
        nc.scalar.activation(warm[:, 1:2], warm[:, 0:1], ACT.Sigmoid)

        def weight_tiles(name):
            staged = [sb("%s_bf%d" % (name, u), [P, 2, P, PACK], BF16) for u in range(2)]
            return staged, sb(name + "_codes", [P, 512], U32), sb(name + "_scales", [P, 512], U8)

        def cast_weight(copy, wt, raw, u, m0):
            count = raw.shape[2] // PACK
            copy(
                out=wt[0][u][:, :, m0 : m0 + count, :].rearrange("p t m j -> p m j t"),
                in_=raw[:].rearrange("p j (m t) -> p m j t", t=PACK)[:, :, :, 2 * u : 2 * u + 2],
            )

        def quant_weight(wt, u):
            cols = slice(u * 256, (u + 1) * 256)
            nc.vector.quantize_mx(
                out=wt[1][:, cols].bitcast(FP8X4), scales=wt[2][:, cols],
                in_=wt[0][u][:].rearrange("p t m j -> p (t m j)"),
            )

        def product(acc, wt, t, codes, scales, start, stop):
            cols = slice(t * P, (t + 1) * P)
            nc.tensor.matmul_mx(
                out=acc, lhsT=wt[1][:, cols].bitcast(FP8X4), lhsT_scale=wt[2][:, cols],
                rhs=codes.bitcast(FP8X4), rhs_scale=scales, start=start, stop=stop,
            )

        xq_w = sb("xq_w", [P, S], U32)
        xq_s = sb("xq_s", [P, S], U8)
        xh_w = sb("xh_w", [P, S], U32)
        xh_g = sb("xh_g", [P, S], U8)
        xh_s = sb("xh_s", [P, S], U8)
        nc.vector.tensor_copy(xq_s[:], xs[:].indirect(l_offs[:]))
        nc.vector.tensor_copy(xh_g[:], xs[:].indirect(l_hz[:]))
        wt1 = weight_tiles("w1")
        for q in range(2):
            for u in range(2):
                cast_weight(nc.scalar.copy, wt1, w1_raw[q], u, 64 * q)
        quant_weight(wt1, 0)
        nc.vector.tensor_copy(xh_s[:].bitcast(I32), xh_g[:].bitcast(I32))
        quant_weight(wt1, 1)
        banks = [psum.tile([P, S], F32, name="y_ps%d" % t, tag="bank%d" % t) for t in range(PACK)]
        y_ps = {t: [] for t in range(PACK)}
        for half in range(2):
            cols = slice(half * HALF, (half + 1) * HALF)
            nc.vector.tensor_copy(xq_w[:, cols], xw[:].bitcast(U32).indirect(entries(l_offs, half * HALF, HALF)))
            for t in range(2):
                acc = banks[half][:, t * HALF : (t + 1) * HALF]
                product(acc, wt1, t, xq_w[:, cols], xq_s[:, cols], True, True)
                y_ps[t].append((cols, acc))
        for t in range(2, PACK):
            product(banks[t][:], wt1, t, xq_w[:], xq_s[:], True, True)
            y_ps[t].append((slice(0, S), banks[t][:]))
        nc.vector.tensor_copy(xh_w[:], xw[:].bitcast(U32).indirect(l_hz[:]))
        for r in range(2):
            nc.sync.dma_start(out=xh_s[2 + r : P : 32, :].bitcast(I32), in_=xh_g[16 + r : P : 32, :].bitcast(I32))
        gn_sb = sb("gn_sb", [P, PACK], F32)
        gm_sb = sb("gm_sb", [P, PACK], F32)
        l_n1 = load_list("l_n1", n1)
        nc.sync.dma_start(out=gm_sb[:], in_=gm.rearrange("(p t) o -> p (t o)", t=PACK))
        nc.sync.dma_start(out=gn_sb[:], in_=gn.rearrange("(p t) o -> p (t o)", t=PACK))
        w3_raw = load_weight("w3_raw", w3, 0, N)
        l_n3 = load_list("l_n3", n3)
        l_n4 = load_list("l_n4", n4)
        w4_raw = load_weight("w4_raw", w4, 0, N)
        l_n5 = load_list("l_n5", n5)

        gm_abs = sb("gm_abs", [P, PACK], F32)
        gm_sign = sb("gm_sign", [P, PACK], BF16)
        nc.scalar.activation(gm_abs[:], gm_sb[:], ACT.Abs)
        nc.scalar.activation(gm_sign[:], gm_sb[:], ACT.Sign)

        wt2 = weight_tiles("w2")
        for q in range(2):
            for u in range(2):
                cast_weight(nc.vector.tensor_copy, wt2, w2_raw[q], u, 64 * q)
        quant_weight(wt2, 0)
        quant_weight(wt2, 1)
        d_ps = [psum.tile([P, S], F32, name="d_ps%d" % t, tag="bank%d" % (PACK + t)) for t in range(PACK)]
        for t in range(PACK):
            product(d_ps[t][:], wt2, t, xh_w[:], xh_s[:], True, True)

        y_sb = [sb("y_sb%d" % t, [P, 2 * S], F32) for t in range(PACK)]
        y2 = [sb("y2_%d" % t, [P, S], F32) for t in range(PACK)]
        diff = [sb("diff%d" % t, [P, S], F32) for t in range(PACK)]
        sig = [sb("sig%d" % t, [P, S], F32) for t in range(PACK)]
        z_planes = sb("z_planes", [P, PACK, S], BF16)
        d_sb = [sb("d_sb%d" % t, [P, S], F32) for t in range(PACK)]

        def fetch_y(t):
            if t >= 2:
                (nc.vector.tensor_copy if t in YV else nc.scalar.copy)(out=y_sb[t][:, :S], in_=banks[t][:])
            nc.scalar.activation(y2[t][:], y_sb[t][:].indirect(l_n2[:]), ACT.Copy)
            nc.vector.tensor_tensor(diff[t][:], y_sb[t][:].indirect(l_n1[:]), y2[t][:], ALU.subtract)

        def gate_y(t):
            nc.scalar.activation(sig[t][:], diff[t][:], ACT.Sigmoid)
            nc.vector.scalar_tensor_tensor(
                z_planes[:, t, :], y_sb[t][:, :S], gn_sb[:, t : t + 1], sig[t][:], ALU.mult, ALU.mult
            )

        def leave_d(t):
            nc.scalar.activation(d_sb[t][:], d_ps[t][:], ACT.Copy, scale=gm_abs[:, t : t + 1])

        for half in range(2):
            for t in range(2):
                cols, acc = y_ps[t][half]
                nc.scalar.copy(out=y_sb[t][:, cols], in_=acc)
        for t in range(PACK):
            fetch_y(t)
        for t in range(PACK):
            gate_y(t)
            leave_d(t)

        z_codes = sb("z_codes", [P, S], U32)
        z_scales = sb("z_scales", [P, S], U8)
        wt3 = weight_tiles("w3")
        wt4 = weight_tiles("w4")
        for wt, raw in ((wt3, w3_raw), (wt4, w4_raw)):
            for u in range(2):
                cast_weight(nc.vector.tensor_copy, wt, raw, u, 0)
            for u in range(2):
                quant_weight(wt, u)

        h_neg = [sb("h_neg%d" % t, [P, S], F32) for t in range(PACK)]
        h_twin = [sb("h_twin%d" % t, [P, HALF], F32) for t in range(PACK)]
        z2_codes = sb("z2_codes", [P, S], U32)
        z2_scales = sb("z2_scales", [P, S], U8)
        h_ps = {}
        free_banks = [0, 1, 2, 3, 4, 5, 6, 7]

        def make_z2(c0, width):
            cols = slice(c0, c0 + width)
            d3 = sb("d3_%d" % c0, [P, PACK, width], F32)
            d4 = sb("d4_%d" % c0, [P, PACK, width], F32)
            big = sb("big_%d" % c0, [P, PACK, width], F32)
            woven = sb("z2_woven%d" % c0, [P, width, PACK], BF16)
            signed = sb("z2_signed%d" % c0, [P, width, PACK], BF16)
            for t in range(PACK):
                nc.scalar.activation(d3[:, t, :], d_sb[t][:].indirect(entries(l_n3, c0, width)), ACT.Copy)
                nc.vector.scalar_tensor_tensor(
                    big[:, t, :], d_ps[t][:, cols], gm_abs[:, t : t + 1], d3[:, t, :], ALU.mult, ALU.max
                )
            for t in range(PACK):
                nc.scalar.activation(d4[:, t, :], d_sb[t][:].indirect(entries(l_n4, c0, width)), ACT.Copy)
            nc.vector.tensor_tensor(
                woven[:].rearrange("p (c i) t -> p c t i", i=2),
                big[:].rearrange("p t (c i) -> p c t i", i=2),
                d4[:].rearrange("p t (c i) -> p c t i", i=2),
                ALU.min,
            )
            z_woven = sb("z_woven%d" % c0, [P, width, PACK], BF16)
            (nc.scalar.copy if c0 in ZS else nc.vector.tensor_copy)(
                out=z_woven[:].rearrange("p (c i) t -> p c t i", i=4),
                in_=z_planes[:, :, cols].rearrange("p t (c i) -> p c t i", i=4),
            )
            nc.vector.tensor_tensor(
                signed[:], woven[:], gm_sign[:].unsqueeze(1).to_broadcast([P, width, PACK]), ALU.mult
            )
            nc.vector.quantize_mx(
                out=z_codes[:, cols].bitcast(FP8X4), scales=z_scales[:, cols],
                in_=z_woven[:].rearrange("p j t -> p (j t)"),
            )
            nc.vector.quantize_mx(
                out=z2_codes[:, cols].bitcast(FP8X4), scales=z2_scales[:, cols],
                in_=signed[:].rearrange("p j t -> p (j t)"),
            )
            for pair in ((0, 1), (2, 3)) if c0 + width < S else ((0,), (1,), (2,), (3,)):
                bank = psum.tile([P, len(pair), width], F32, name="h_ps%d_%d" % (c0, pair[0]), tag="bank%d" % free_banks.pop(0))
                for k, t in enumerate(pair):
                    product(bank[:, k, :], wt3, t, z_codes[:, cols], z_scales[:, cols], k == 0, False)
                for k, t in enumerate(pair):
                    product(bank[:, k, :], wt4, t, z2_codes[:, cols], z2_scales[:, cols], False, k == len(pair) - 1)
                    h_ps[c0, t] = bank[:, k, :]

        def leave_h(c0, width):
            for t in range(PACK):
                nc.scalar.activation(h_neg[t][:, c0 : c0 + width], h_ps[c0, t], ACT.Copy, scale=-1.0)

        for piece in PIECES:
            make_z2(*piece)
        for piece in PIECES:
            leave_h(*piece)
        for t in range(PACK):
            nc.sync.dma_start(out=h_twin[t][:], in_=h_neg[t][:, :HALF])

        out_rows = out.rearrange("(p t) n -> p t n", t=PACK)
        for t in range(PACK):
            low = sb("low%d" % t, [P, HALF], F32)
            high = sb("high%d" % t, [P, HALF], F32)
            h5 = sb("h5_%d" % t, [P, HALF], F32)
            nc.vector.tensor_tensor(low[:], h_neg[t][:].indirect(entries(l_n5, 0, HALF)), h_twin[t][:], ALU.subtract)
            nc.sync.dma_start(out=out_rows[:, t, :HALF], in_=low[:])
            nc.scalar.activation(h5[:], h_neg[t][:].indirect(entries(l_n5, HALF, HALF)), ACT.Copy)
            nc.vector.tensor_tensor(high[:], h5[:], h_neg[t][:, HALF:], ALU.subtract)
            nc.sync.dma_start(out=out_rows[:, t, HALF:], in_=high[:])
